import numpy as np, ml_dtypes
CORES = [83,85,87,115,117,119]
N = 6
import mx_ref
NC, G = 128, 4
C = np.float32(0.029)
BF = ml_dtypes.bfloat16
def cut(t, i, w=512):
    return t[:, w * i:w * i + w]
def tile(rs):
    return np.stack(rs, axis=2).reshape(128, -1).astype(BF)
def layer(w, X):
    out = []
    for i in range(G):
        for t in range(len(X)):
            p = mx_ref.matmul(mx_ref.quantize(cut(w, len(X) * i + t)), X[t])
            z = p if t == 0 else z + p
        out.append(z)
    return out
def masked(A, E):
    return [(e * (a > 0)) * C for a, e in zip(A, E)]
def setup_inputs(rng):
    def f(*shape):
        return mx_ref.flush((rng.standard_normal(shape, dtype=np.float32) * np.exp2(rng.integers(-2, 3, shape[:-1] + (1,)))).astype(BF))
    return {"x": f(N, 128, 512), "e": f(N, 128, 512), "a": f(N, 128, G * 512), "w": f(N, 128, 512), "v": f(N, 128, 4 * NC)}
def setup_inputs_blocks(rng):
    d = setup_inputs(rng)
    for k in ("x", "e", "a", "w", "v"): d[k] = mx_ref.spread(d[k], rng, 2)
    return d
def setup_inputs_wide(rng):
    d = setup_inputs(rng)
    for k in ("x", "e", "a", "w", "v"): d[k] = mx_ref.flush((d[k].astype(np.float32) * np.exp2(rng.integers(-6, 7, (N, 1, 1))).astype(np.float32)).astype(BF))
    return d
def setup_inputs_zeros(rng):
    d = setup_inputs(rng); v = d["x"].reshape(N, 128, -1, 4).copy()
    v[np.broadcast_to((rng.random((N, 1, v.shape[2], 1)) < 0.33), v.shape)] = 0
    d["x"] = v.reshape(d["x"].shape)
    return d
def reference(x, e, a, w, v):
    T = [mx_ref.quantize(tile(masked(layer(a[j], [mx_ref.quantize(x[j])]), layer(a[j], [mx_ref.quantize(e[j])])))) for j in range(N)]
    y = np.zeros((N, 128, N * 128), np.float32); z = np.zeros((N, 128, NC), np.float32)
    for r in range(N):
        qw = mx_ref.quantize(w[r]); qv = mx_ref.quantize(v[r])
        for j in range(N):
            y[r][:, 128 * j:128 * j + 128] = mx_ref.matmul(qw, T[j])
            p = mx_ref.matmul(T[j], qv)
            z[r] = p if j == 0 else z[r] + p
    return {"y": y, "z": z}

@@ -1,0 +1,152 @@
+from concourse.bass import DstId, RemoteDMATransfer
+from concourse.mybir import dt, AluOpType, ActivationFunctionType
+
+N = 6
+B = 128
+G = 4
+BANK = 512
+SCALE = 0.029
+
+F8 = "float8_e4m3fn_x4"
+SCRATCH = {
+    "xe": ("sbuf", [128, 8 * B], "bfloat16"),
+    "ab": ("sbuf", [128, 4 * B * G], "bfloat16"),
+    "wv": ("sbuf", [128, 8 * B], "bfloat16"),
+    "tb": ("sbuf", [128, 4 * B], "bfloat16"),
+    "qxe": ("sbuf", [128, 2 * B], F8), "sxe": ("sbuf", [128, 2 * B], "uint8"),
+    "qa": ("sbuf", [128, G * B], F8), "sa": ("sbuf", [128, G * B], "uint8"),
+    "qwv": ("sbuf", [128, 2 * B], F8), "swv": ("sbuf", [128, 2 * B], "uint8"),
+    "qt": ("sbuf", [128, N * B], F8), "st": ("sbuf", [128, N * B], "uint8"),
+    "mk": ("sbuf", [128, G * B], "float32"),
+    "ysb": ("sbuf", [128, N * B], "float32"),
+    "zsb": ("sbuf", [128, B], "float32"),
+    "ps": ("psum", [128, 8 * BANK], "float32"),
+}
+SEMAPHORES = (["l_xe", "l_a0", "l_a1", "l_wv", "q_xe", "q_wv", "q_t", "sent", "zmm", "zcp", "st_sy", "st_sc"]
+              + ["q_a%d" % i for i in range(G)] + ["mm%d" % i for i in range(G)]
+              + ["mk%d" % i for i in range(G)] + ["tb%d" % i for i in range(G)]
+              + ["arr%d" % j for j in range(N)] + ["ymm%d" % j for j in range(N)] + ["ycp%d" % j for j in range(N)])
+
+
+def _popcount(m):
+    return bin(m).count("1")
+
+
+def _cols(j, w=B):
+    return slice(j * w, (j + 1) * w)
+
+
+def rank_program(g, core, T, topo):
+    me = T.rank_of(core)
+    if me is None:
+        return
+    sem = T.sem
+    cores = T.cores
+    here = [r for r in range(N) if topo.chip(cores[r]) == topo.chip(core)]
+    peers = [r for r in here if r != me]
+    far = [r for r in range(N) if r not in here]
+
+    def port_mates(r):
+        return sum(1 for s in range(N) if topo.chip(cores[s]) == topo.chip(cores[r]) and topo.die(cores[s]) == topo.die(cores[r]))
+    far_in = sorted(far, key=lambda r: (port_mates(r), r))
+    order = [me] + peers + far_in
+
+    far_mask = 0xFFFFFFFF
+    for r in far:
+        far_mask &= topo.mask(core, cores[r])
+    near_mask = 0xFFFFFFFF
+    for r in peers:
+        near_mask &= topo.mask(core, cores[r])
+    near_mask &= ~far_mask
+
+    def dst(r):
+        rid, pid, _s = topo.addr(cores[r])
+        return DstId(rid=rid, pnc=pid)
+
+    g.sync.dma_start(T.xe[:, 0:4 * B], T.x[:]).then_inc(sem["l_xe"], 16)
+    g.scalar.dma_start(T.xe[:, 4 * B:8 * B], T.e[:]).then_inc(sem["l_xe"], 16)
+    g.sync.dma_start(T.ab[:, 0:8 * B], T.a[:, 0:8 * B]).then_inc(sem["l_a0"], 16)
+    g.scalar.dma_start(T.ab[:, 8 * B:16 * B], T.a[:, 8 * B:16 * B]).then_inc(sem["l_a1"], 16)
+    g.sync.dma_start(T.wv[:, 0:4 * B], T.w[:]).then_inc(sem["l_wv"], 16)
+    g.scalar.dma_start(T.wv[:, 4 * B:8 * B], T.v[:]).then_inc(sem["l_wv"], 16)
+
+    v = g.vector
+    v.wait_ge(sem["l_xe"], 32)
+    v.quantize_mx(T.qxe[:, :], T.sxe[:, :], T.xe[:, :]).then_inc(sem["q_xe"], 1)
+    for half in range(2):
+        v.wait_ge(sem["l_a%d" % half], 16)
+        pair = (2 * half, 2 * half + 1)
+        for i in pair:
+            v.quantize_mx(T.qa[:, _cols(i)], T.sa[:, _cols(i)], T.ab[:, _cols(i, 4 * B)]).then_inc(sem["q_a%d" % i], 1)
+        for i in pair:
+            u = T.ps[:, i * BANK:i * BANK + B]
+            d = T.ps[:, i * BANK + B:i * BANK + 2 * B]
+            v.wait_ge(sem["mm%d" % i], 1)
+            v.tensor_scalar(T.mk[:, _cols(i)], u, 0.0, SCALE, AluOpType.is_gt, AluOpType.mult).then_inc(sem["mk%d" % i], 1)
+            v.wait_ge(sem["mk%d" % i], 1)
+            v.tensor_tensor(T.tb[:, i:4 * B:4], d, T.mk[:, _cols(i)], AluOpType.mult).then_inc(sem["tb%d" % i], 1)
+    for i in range(G):
+        v.wait_ge(sem["tb%d" % i], 1)
+    v.quantize_mx(T.qt[:, _cols(me)], T.st[:, _cols(me)], T.tb[:, :]).then_inc(sem["q_t"], 1)
+    v.wait_ge(sem["l_wv"], 32)
+    v.quantize_mx(T.qwv[:, :], T.swv[:, :], T.wv[:, :]).then_inc(sem["q_wv"], 1)
+
+    t = g.tensor
+    t.wait_ge(sem["q_xe"], 1)
+    for i in range(G):
+        t.wait_ge(sem["q_a%d" % i], 1)
+        t.matmul_mx(T.ps[:, i * BANK:i * BANK + 2 * B], T.qa[:, _cols(i)], T.sa[:, _cols(i)],
+                    T.qxe[:, :], T.sxe[:, :], True, True).then_inc(sem["mm%d" % i], 1)
+    t.wait_ge(sem["q_t"], 1)
+    t.wait_ge(sem["q_wv"], 1)
+    zb = 7 * BANK
+    ybank = [4, 5, 6, 0, 1, 2]
+    arrivals = 2 * _popcount(near_mask), 2 * _popcount(far_mask)
+    for k, j in enumerate(order):
+        if j != me:
+            t.wait_ge(sem["arr%d" % j], arrivals[0] if j in here else arrivals[1])
+        yb = ybank[k] * BANK
+        t.matmul_mx(T.ps[:, yb:yb + B], T.qwv[:, 0:B], T.swv[:, 0:B],
+                    T.qt[:, _cols(j)], T.st[:, _cols(j)], True, True).then_inc(sem["ymm%d" % j], 1)
+        last = k == N - 1
+        m = t.matmul_mx(T.ps[:, zb:zb + B], T.qt[:, _cols(j)], T.st[:, _cols(j)],
+                        T.qwv[:, B:2 * B], T.swv[:, B:2 * B], k == 0, last)
+        if last:
+            m.then_inc(sem["zmm"], 1)
+
+    mine_q = T.qt[:, _cols(me)].bitcast(dt.uint8)
+    mine_s = T.st[:, _cols(me)]
+    arr = sem["arr%d" % me]
+
+    def send(ranks, mask, what):
+        return RemoteDMATransfer(dst_ids=[dst(r) for r in ranks], dma_engine_mask=mask, remote_sem=arr,
+                                 srcs=[what], dsts=[what for _ in ranks])
+    g.wait_ge(sem["q_t"], 1)
+    g.remote_dma_fused([send(far, far_mask, mine_q)], local_sem=sem["sent"])
+    g.remote_dma_fused([send(peers, near_mask, mine_q)], local_sem=sem["sent"])
+    g.remote_dma_fused([send(far, far_mask, mine_s), send(peers, near_mask, mine_s)], local_sem=sem["sent"])
+
+    for k, j in enumerate(order):
+        yb = ybank[k] * BANK
+        v.wait_ge(sem["ymm%d" % j], 1)
+        v.tensor_copy(T.ysb[:, _cols(j)], T.ps[:, yb:yb + B]).then_inc(sem["ycp%d" % j], 1)
+
+    lo, hi = here[0], here[-1] + 1
+    for j in here:
+        g.sync.wait_ge(sem["ycp%d" % j], 1)
+    g.sync.dma_start(T.y[:, lo * B:hi * B], T.ysb[:, lo * B:hi * B]).then_inc(sem["st_sy"], 16)
+    stores = 1
+    g.scalar.wait_ge(sem["ycp%d" % far_in[0]], 1)
+    g.scalar.dma_start(T.y[:, _cols(far_in[0])], T.ysb[:, _cols(far_in[0])]).then_inc(sem["st_sc"], 16)
+    for j in far_in[1:]:
+        g.sync.wait_ge(sem["ycp%d" % j], 1)
+        g.sync.dma_start(T.y[:, _cols(j)], T.ysb[:, _cols(j)]).then_inc(sem["st_sy"], 16)
+        stores += 1
+    g.scalar.wait_ge(sem["zmm"], 1)
+    g.scalar.activation(T.zsb[:, :], T.ps[:, zb:zb + B], ActivationFunctionType.Copy).then_inc(sem["zcp"], 1)
+    g.scalar.wait_ge(sem["zcp"], 1)
+    g.scalar.dma_start(T.z[:, :], T.zsb[:, :]).then_inc(sem["st_sc"], 16)
+
+    g.sync.wait_ge(sem["st_sy"], 16 * stores)
+    g.scalar.wait_ge(sem["st_sc"], 32)
+    g.wait_ge(sem["sent"], 2 * _popcount(far_mask) + 2 * _popcount(near_mask))

@@ -23,9 +23,10 @@ SCRATCH = {
     "ps": ("psum", [128, 8 * BANK], "float32"),
 }
 SEMAPHORES = (["l_xe", "l_a0", "l_a1", "l_wv", "q_xe", "q_wv", "q_t", "sent", "zmm", "zcp", "st_sy", "st_sc"]
-              + ["q_a%d" % i for i in range(G)] + ["mm%d" % i for i in range(G)]
+              + ["q_a%d" % i for i in range(G)] + ["mu%d" % i for i in range(G)] + ["md%d" % i for i in range(G)]
               + ["mk%d" % i for i in range(G)] + ["tb%d" % i for i in range(G)]
-              + ["arr%d" % j for j in range(N)] + ["ymm%d" % j for j in range(N)] + ["ycp%d" % j for j in range(N)])
+              + ["arrq%d" % j for j in range(N)] + ["arrs%d" % j for j in range(N)]
+              + ["ymm%d" % j for j in range(N)] + ["ycp%d" % j for j in range(N)])
 
 
 def _popcount(m):
@@ -42,22 +43,29 @@ def rank_program(g, core, T, topo):
         return
     sem = T.sem
     cores = T.cores
-    here = [r for r in range(N) if topo.chip(cores[r]) == topo.chip(core)]
-    peers = [r for r in here if r != me]
-    far = [r for r in range(N) if r not in here]
 
-    def port_mates(r):
-        return sum(1 for s in range(N) if topo.chip(cores[s]) == topo.chip(cores[r]) and topo.die(cores[s]) == topo.die(cores[r]))
-    far_in = sorted(far, key=lambda r: (port_mates(r), r))
+    def chip_ranks(r, same):
+        return [s for s in range(N) if (topo.chip(cores[s]) == topo.chip(cores[r])) == same]
+
+    def far_order(r):
+        f, k = chip_ranks(r, False), chip_ranks(r, True).index(r)
+        return f[k:] + f[:k]
+    here = chip_ranks(me, True)
+    peers = [r for r in here if r != me]
+    relay, second, _third = far_order(me)
+    far_in = sorted(far_order(me), key=lambda r: far_order(r).index(me))
+    mine_to_relay = far_in[0]
+    relay_to = far_order(mine_to_relay)[2]
     order = [me] + peers + far_in
 
     far_mask = 0xFFFFFFFF
-    for r in far:
+    for r in far_in:
         far_mask &= topo.mask(core, cores[r])
     near_mask = 0xFFFFFFFF
     for r in peers:
         near_mask &= topo.mask(core, cores[r])
     near_mask &= ~far_mask
+    n_far, n_near = _popcount(far_mask), _popcount(near_mask)
 
     def dst(r):
         rid, pid, _s = topo.addr(cores[r])
@@ -70,6 +78,9 @@ def rank_program(g, core, T, topo):
     g.sync.dma_start(T.wv[:, 0:4 * B], T.w[:]).then_inc(sem["l_wv"], 16)
     g.scalar.dma_start(T.wv[:, 4 * B:8 * B], T.v[:]).then_inc(sem["l_wv"], 16)
 
+    def bank(k):
+        return T.ps[:, k * BANK:k * BANK + B]
+
     v = g.vector
     v.wait_ge(sem["l_xe"], 32)
     v.quantize_mx(T.qxe[:, :], T.sxe[:, :], T.xe[:, :]).then_inc(sem["q_xe"], 1)
@@ -79,12 +90,11 @@ def rank_program(g, core, T, topo):
         for i in pair:
             v.quantize_mx(T.qa[:, _cols(i)], T.sa[:, _cols(i)], T.ab[:, _cols(i, 4 * B)]).then_inc(sem["q_a%d" % i], 1)
         for i in pair:
-            u = T.ps[:, i * BANK:i * BANK + B]
-            d = T.ps[:, i * BANK + B:i * BANK + 2 * B]
-            v.wait_ge(sem["mm%d" % i], 1)
-            v.tensor_scalar(T.mk[:, _cols(i)], u, 0.0, SCALE, AluOpType.is_gt, AluOpType.mult).then_inc(sem["mk%d" % i], 1)
+            v.wait_ge(sem["mu%d" % i], 1)
+            v.tensor_scalar(T.mk[:, _cols(i)], bank(i), 0.0, SCALE, AluOpType.is_gt, AluOpType.mult).then_inc(sem["mk%d" % i], 1)
+            v.wait_ge(sem["md%d" % i], 1)
             v.wait_ge(sem["mk%d" % i], 1)
-            v.tensor_tensor(T.tb[:, i:4 * B:4], d, T.mk[:, _cols(i)], AluOpType.mult).then_inc(sem["tb%d" % i], 1)
+            v.tensor_tensor(T.tb[:, i:4 * B:4], bank(G + i), T.mk[:, _cols(i)], AluOpType.mult).then_inc(sem["tb%d" % i], 1)
     for i in range(G):
         v.wait_ge(sem["tb%d" % i], 1)
     v.quantize_mx(T.qt[:, _cols(me)], T.st[:, _cols(me)], T.tb[:, :]).then_inc(sem["q_t"], 1)
@@ -95,41 +105,43 @@ def rank_program(g, core, T, topo):
     t.wait_ge(sem["q_xe"], 1)
     for i in range(G):
         t.wait_ge(sem["q_a%d" % i], 1)
-        t.matmul_mx(T.ps[:, i * BANK:i * BANK + 2 * B], T.qa[:, _cols(i)], T.sa[:, _cols(i)],
-                    T.qxe[:, :], T.sxe[:, :], True, True).then_inc(sem["mm%d" % i], 1)
+        for k, s in ((0, "mu%d" % i), (1, "md%d" % i)):
+            t.matmul_mx(bank(G * k + i), T.qa[:, _cols(i)], T.sa[:, _cols(i)],
+                        T.qxe[:, _cols(k)], T.sxe[:, _cols(k)], True, True).then_inc(sem[s], 1)
     t.wait_ge(sem["q_t"], 1)
     t.wait_ge(sem["q_wv"], 1)
-    zb = 7 * BANK
-    ybank = [4, 5, 6, 0, 1, 2]
-    arrivals = 2 * _popcount(near_mask), 2 * _popcount(far_mask)
+    zbank = N
+    direct = far_in[:2]
     for k, j in enumerate(order):
         if j != me:
-            t.wait_ge(sem["arr%d" % j], arrivals[0] if j in here else arrivals[1])
-        yb = ybank[k] * BANK
-        t.matmul_mx(T.ps[:, yb:yb + B], T.qwv[:, 0:B], T.swv[:, 0:B],
+            t.wait_ge(sem["arrq%d" % j], n_far if j in direct else n_near)
+            t.wait_ge(sem["arrs%d" % j], n_far if j in direct else n_near)
+        t.matmul_mx(bank(k), T.qwv[:, 0:B], T.swv[:, 0:B],
                     T.qt[:, _cols(j)], T.st[:, _cols(j)], True, True).then_inc(sem["ymm%d" % j], 1)
         last = k == N - 1
-        m = t.matmul_mx(T.ps[:, zb:zb + B], T.qt[:, _cols(j)], T.st[:, _cols(j)],
+        m = t.matmul_mx(bank(zbank), T.qt[:, _cols(j)], T.st[:, _cols(j)],
                         T.qwv[:, B:2 * B], T.swv[:, B:2 * B], k == 0, last)
         if last:
             m.then_inc(sem["zmm"], 1)
 
-    mine_q = T.qt[:, _cols(me)].bitcast(dt.uint8)
-    mine_s = T.st[:, _cols(me)]
-    arr = sem["arr%d" % me]
-
-    def send(ranks, mask, what):
-        return RemoteDMATransfer(dst_ids=[dst(r) for r in ranks], dma_engine_mask=mask, remote_sem=arr,
-                                 srcs=[what], dsts=[what for _ in ranks])
+    def send(kind, j, ranks, mask):
+        what = T.qt[:, _cols(j)].bitcast(dt.uint8) if kind == "q" else T.st[:, _cols(j)]
+        g.remote_dma_fused([RemoteDMATransfer(dst_ids=[dst(r) for r in ranks], dma_engine_mask=mask,
+                                              remote_sem=sem["arr%s%d" % (kind, j)],
+                                              srcs=[what], dsts=[what for _ in ranks])], local_sem=sem["sent"])
     g.wait_ge(sem["q_t"], 1)
-    g.remote_dma_fused([send(far, far_mask, mine_q)], local_sem=sem["sent"])
-    g.remote_dma_fused([send(peers, near_mask, mine_q)], local_sem=sem["sent"])
-    g.remote_dma_fused([send(far, far_mask, mine_s), send(peers, near_mask, mine_s)], local_sem=sem["sent"])
+    for r in (relay, second):
+        send("q", me, [r], far_mask)
+        send("s", me, [r], far_mask)
+    send("q", me, peers, near_mask)
+    send("s", me, peers, near_mask)
+    for kind in ("q", "s"):
+        g.wait_ge(sem["arr%s%d" % (kind, mine_to_relay)], n_far)
+        send(kind, mine_to_relay, [relay_to], near_mask)
 
     for k, j in enumerate(order):
-        yb = ybank[k] * BANK
         v.wait_ge(sem["ymm%d" % j], 1)
-        v.tensor_copy(T.ysb[:, _cols(j)], T.ps[:, yb:yb + B]).then_inc(sem["ycp%d" % j], 1)
+        v.tensor_copy(T.ysb[:, _cols(j)], bank(k)).then_inc(sem["ycp%d" % j], 1)
 
     lo, hi = here[0], here[-1] + 1
     for j in here:
@@ -143,10 +155,10 @@ def rank_program(g, core, T, topo):
         g.sync.dma_start(T.y[:, _cols(j)], T.ysb[:, _cols(j)]).then_inc(sem["st_sy"], 16)
         stores += 1
     g.scalar.wait_ge(sem["zmm"], 1)
-    g.scalar.activation(T.zsb[:, :], T.ps[:, zb:zb + B], ActivationFunctionType.Copy).then_inc(sem["zcp"], 1)
+    g.scalar.activation(T.zsb[:, :], bank(zbank), ActivationFunctionType.Copy).then_inc(sem["zcp"], 1)
     g.scalar.wait_ge(sem["zcp"], 1)
     g.scalar.dma_start(T.z[:, :], T.zsb[:, :]).then_inc(sem["st_sc"], 16)
 
     g.sync.wait_ge(sem["st_sy"], 16 * stores)
     g.scalar.wait_ge(sem["st_sc"], 32)
-    g.wait_ge(sem["sent"], 2 * _popcount(far_mask) + 2 * _popcount(near_mask))
+    g.wait_ge(sem["sent"], 4 * n_far + 4 * n_near)

@@ -53,19 +53,14 @@ def rank_program(g, core, T, topo):
     here = chip_ranks(me, True)
     peers = [r for r in here if r != me]
     relay, second, _third = far_order(me)
-    far_in = sorted(far_order(me), key=lambda r: far_order(r).index(me))
-    mine_to_relay = far_in[0]
-    relay_to = far_order(mine_to_relay)[2]
-    order = [me] + peers + far_in
+    to_relay, direct, relayed = sorted(far_order(me), key=lambda r: far_order(r).index(me))
+    relay_to = far_order(to_relay)[2]
+    order = [me, to_relay] + peers + [direct, relayed]
 
-    far_mask = 0xFFFFFFFF
-    for r in far_in:
-        far_mask &= topo.mask(core, cores[r])
-    near_mask = 0xFFFFFFFF
-    for r in peers:
-        near_mask &= topo.mask(core, cores[r])
-    near_mask &= ~far_mask
-    n_far, n_near = _popcount(far_mask), _popcount(near_mask)
+    far_mask = topo.mask(core, cores[relay]) & topo.mask(core, cores[second])
+    all_mask = topo.mask(core, cores[relay_to])
+    near_mask = all_mask & ~far_mask
+    n_far, n_near, n_all = _popcount(far_mask), _popcount(near_mask), _popcount(all_mask)
 
     def dst(r):
         rid, pid, _s = topo.addr(cores[r])
@@ -85,15 +80,16 @@ def rank_program(g, core, T, topo):
     v.wait_ge(sem["l_xe"], 32)
     v.quantize_mx(T.qxe[:, :], T.sxe[:, :], T.xe[:, :]).then_inc(sem["q_xe"], 1)
     for half in range(2):
-        v.wait_ge(sem["l_a%d" % half], 16)
         pair = (2 * half, 2 * half + 1)
+        v.wait_ge(sem["l_a%d" % half], 16)
         for i in pair:
             v.quantize_mx(T.qa[:, _cols(i)], T.sa[:, _cols(i)], T.ab[:, _cols(i, 4 * B)]).then_inc(sem["q_a%d" % i], 1)
         for i in pair:
             v.wait_ge(sem["mu%d" % i], 1)
             v.tensor_scalar(T.mk[:, _cols(i)], bank(i), 0.0, SCALE, AluOpType.is_gt, AluOpType.mult).then_inc(sem["mk%d" % i], 1)
-            v.wait_ge(sem["md%d" % i], 1)
+        for i in pair:
             v.wait_ge(sem["mk%d" % i], 1)
+            v.wait_ge(sem["md%d" % i], 1)
             v.tensor_tensor(T.tb[:, i:4 * B:4], bank(G + i), T.mk[:, _cols(i)], AluOpType.mult).then_inc(sem["tb%d" % i], 1)
     for i in range(G):
         v.wait_ge(sem["tb%d" % i], 1)
@@ -103,19 +99,23 @@ def rank_program(g, core, T, topo):
 
     t = g.tensor
     t.wait_ge(sem["q_xe"], 1)
-    for i in range(G):
-        t.wait_ge(sem["q_a%d" % i], 1)
-        for k, s in ((0, "mu%d" % i), (1, "md%d" % i)):
-            t.matmul_mx(bank(G * k + i), T.qa[:, _cols(i)], T.sa[:, _cols(i)],
-                        T.qxe[:, _cols(k)], T.sxe[:, _cols(k)], True, True).then_inc(sem[s], 1)
+    for half in range(2):
+        pair = (2 * half, 2 * half + 1)
+        for k, s in ((0, "mu%d"), (1, "md%d")):
+            for i in pair:
+                if k == 0:
+                    t.wait_ge(sem["q_a%d" % i], 1)
+                t.matmul_mx(bank(G * k + i), T.qa[:, _cols(i)], T.sa[:, _cols(i)],
+                            T.qxe[:, _cols(k)], T.sxe[:, _cols(k)], True, True).then_inc(sem[s % i], 1)
     t.wait_ge(sem["q_t"], 1)
     t.wait_ge(sem["q_wv"], 1)
     zbank = N
-    direct = far_in[:2]
+    lands = {r: n_near for r in peers}
+    lands.update({to_relay: n_far, direct: n_far, relayed: n_all})
     for k, j in enumerate(order):
         if j != me:
-            t.wait_ge(sem["arrq%d" % j], n_far if j in direct else n_near)
-            t.wait_ge(sem["arrs%d" % j], n_far if j in direct else n_near)
+            t.wait_ge(sem["arrq%d" % j], lands[j])
+            t.wait_ge(sem["arrs%d" % j], lands[j])
         t.matmul_mx(bank(k), T.qwv[:, 0:B], T.swv[:, 0:B],
                     T.qt[:, _cols(j)], T.st[:, _cols(j)], True, True).then_inc(sem["ymm%d" % j], 1)
         last = k == N - 1
@@ -124,41 +124,42 @@ def rank_program(g, core, T, topo):
         if last:
             m.then_inc(sem["zmm"], 1)
 
-    def send(kind, j, ranks, mask):
+    sent = [0]
+
+    def send(kind, j, *parts):
         what = T.qt[:, _cols(j)].bitcast(dt.uint8) if kind == "q" else T.st[:, _cols(j)]
         g.remote_dma_fused([RemoteDMATransfer(dst_ids=[dst(r) for r in ranks], dma_engine_mask=mask,
                                               remote_sem=sem["arr%s%d" % (kind, j)],
-                                              srcs=[what], dsts=[what for _ in ranks])], local_sem=sem["sent"])
+                                              srcs=[what], dsts=[what for _ in ranks])
+                            for ranks, mask in parts], local_sem=sem["sent"])
+        sent[0] += sum(_popcount(mask) for _, mask in parts)
     g.wait_ge(sem["q_t"], 1)
-    for r in (relay, second):
-        send("q", me, [r], far_mask)
-        send("s", me, [r], far_mask)
-    send("q", me, peers, near_mask)
-    send("s", me, peers, near_mask)
     for kind in ("q", "s"):
-        g.wait_ge(sem["arr%s%d" % (kind, mine_to_relay)], n_far)
-        send(kind, mine_to_relay, [relay_to], near_mask)
+        send(kind, me, ([relay], far_mask))
+    for kind in ("q", "s"):
+        send(kind, me, ([second], far_mask), (peers, near_mask))
+    for kind in ("q", "s"):
+        g.wait_ge(sem["arr%s%d" % (kind, to_relay)], n_far)
+        send(kind, to_relay, ([relay_to], all_mask))
 
     for k, j in enumerate(order):
         v.wait_ge(sem["ymm%d" % j], 1)
         v.tensor_copy(T.ysb[:, _cols(j)], bank(k)).then_inc(sem["ycp%d" % j], 1)
 
+    g.scalar.wait_ge(sem["ycp%d" % to_relay], 1)
+    g.scalar.dma_start(T.y[:, _cols(to_relay)], T.ysb[:, _cols(to_relay)]).then_inc(sem["st_sc"], 16)
     lo, hi = here[0], here[-1] + 1
     for j in here:
         g.sync.wait_ge(sem["ycp%d" % j], 1)
     g.sync.dma_start(T.y[:, lo * B:hi * B], T.ysb[:, lo * B:hi * B]).then_inc(sem["st_sy"], 16)
-    stores = 1
-    g.scalar.wait_ge(sem["ycp%d" % far_in[0]], 1)
-    g.scalar.dma_start(T.y[:, _cols(far_in[0])], T.ysb[:, _cols(far_in[0])]).then_inc(sem["st_sc"], 16)
-    for j in far_in[1:]:
+    for j in (direct, relayed):
         g.sync.wait_ge(sem["ycp%d" % j], 1)
         g.sync.dma_start(T.y[:, _cols(j)], T.ysb[:, _cols(j)]).then_inc(sem["st_sy"], 16)
-        stores += 1
     g.scalar.wait_ge(sem["zmm"], 1)
     g.scalar.activation(T.zsb[:, :], bank(zbank), ActivationFunctionType.Copy).then_inc(sem["zcp"], 1)
     g.scalar.wait_ge(sem["zcp"], 1)
     g.scalar.dma_start(T.z[:, :], T.zsb[:, :]).then_inc(sem["st_sc"], 16)
 
-    g.sync.wait_ge(sem["st_sy"], 16 * stores)
+    g.sync.wait_ge(sem["st_sy"], 48)
     g.scalar.wait_ge(sem["st_sc"], 32)
-    g.wait_ge(sem["sent"], 4 * n_far + 4 * n_near)
+    g.wait_ge(sem["sent"], sent[0])

from concourse.bass import DstId, RemoteDMATransfer
from concourse.mybir import dt, AluOpType, ActivationFunctionType

N = 6
B = 128
G = 4
BANK = 512
SCALE = 0.029

F8 = "float8_e4m3fn_x4"
SCRATCH = {
    "xe": ("sbuf", [128, 8 * B], "bfloat16"),
    "ab": ("sbuf", [128, 4 * B * G], "bfloat16"),
    "wv": ("sbuf", [128, 8 * B], "bfloat16"),
    "tb": ("sbuf", [128, 4 * B], "bfloat16"),
    "qxe": ("sbuf", [128, 2 * B], F8), "sxe": ("sbuf", [128, 2 * B], "uint8"),
    "qa": ("sbuf", [128, G * B], F8), "sa": ("sbuf", [128, G * B], "uint8"),
    "qwv": ("sbuf", [128, 2 * B], F8), "swv": ("sbuf", [128, 2 * B], "uint8"),
    "qt": ("sbuf", [128, N * B], F8), "st": ("sbuf", [128, N * B], "uint8"),
    "mk": ("sbuf", [128, G * B], "float32"),
    "ysb": ("sbuf", [128, N * B], "float32"),
    "zsb": ("sbuf", [128, B], "float32"),
    "ps": ("psum", [128, 8 * BANK], "float32"),
}
SEMAPHORES = (["l_xe", "l_a0", "l_a1", "l_wv", "q_xe", "q_wv", "q_t", "sent", "zmm", "zcp", "st_sy", "st_sc"]
              + ["q_a%d" % i for i in range(G)] + ["mu%d" % i for i in range(G)] + ["md%d" % i for i in range(G)]
              + ["mk%d" % i for i in range(G)] + ["tb%d" % i for i in range(G)]
              + ["arrq%d" % j for j in range(N)] + ["arrs%d" % j for j in range(N)]
              + ["ymm%d" % j for j in range(N)] + ["ycp%d" % j for j in range(N)])


def _popcount(m):
    return bin(m).count("1")


def _cols(j, w=B):
    return slice(j * w, (j + 1) * w)


def rank_program(g, core, T, topo):
    me = T.rank_of(core)
    if me is None:
        return
    sem = T.sem
    cores = T.cores

    def chip_ranks(r, same):
        return [s for s in range(N) if (topo.chip(cores[s]) == topo.chip(cores[r])) == same]

    def far_order(r):
        f, k = chip_ranks(r, False), chip_ranks(r, True).index(r)
        return f[k:] + f[:k]
    here = chip_ranks(me, True)
    peers = [r for r in here if r != me]
    relay, second, _third = far_order(me)
    to_relay, direct, relayed = sorted(far_order(me), key=lambda r: far_order(r).index(me))
    relay_to = far_order(to_relay)[2]
    order = [me, to_relay] + peers + [direct, relayed]

    far_mask = topo.mask(core, cores[relay]) & topo.mask(core, cores[second])
    all_mask = topo.mask(core, cores[relay_to])
    near_mask = all_mask & ~far_mask
    n_far, n_near, n_all = _popcount(far_mask), _popcount(near_mask), _popcount(all_mask)

    def dst(r):
        rid, pid, _s = topo.addr(cores[r])
        return DstId(rid=rid, pnc=pid)

    g.sync.dma_start(T.xe[:, 0:4 * B], T.x[:]).then_inc(sem["l_xe"], 16)
    g.scalar.dma_start(T.xe[:, 4 * B:8 * B], T.e[:]).then_inc(sem["l_xe"], 16)
    g.sync.dma_start(T.ab[:, 0:8 * B], T.a[:, 0:8 * B]).then_inc(sem["l_a0"], 16)
    g.scalar.dma_start(T.ab[:, 8 * B:16 * B], T.a[:, 8 * B:16 * B]).then_inc(sem["l_a1"], 16)
    g.sync.dma_start(T.wv[:, 0:4 * B], T.w[:]).then_inc(sem["l_wv"], 16)
    g.scalar.dma_start(T.wv[:, 4 * B:8 * B], T.v[:]).then_inc(sem["l_wv"], 16)

    def bank(k):
        return T.ps[:, k * BANK:k * BANK + B]

    v = g.vector
    v.wait_ge(sem["l_xe"], 32)
    v.quantize_mx(T.qxe[:, :], T.sxe[:, :], T.xe[:, :]).then_inc(sem["q_xe"], 1)
    for half in range(2):
        pair = (2 * half, 2 * half + 1)
        v.wait_ge(sem["l_a%d" % half], 16)
        for i in pair:
            v.quantize_mx(T.qa[:, _cols(i)], T.sa[:, _cols(i)], T.ab[:, _cols(i, 4 * B)]).then_inc(sem["q_a%d" % i], 1)
        for i in pair:
            v.wait_ge(sem["mu%d" % i], 1)
            v.tensor_scalar(T.mk[:, _cols(i)], bank(i), 0.0, SCALE, AluOpType.is_gt, AluOpType.mult).then_inc(sem["mk%d" % i], 1)
        for i in pair:
            v.wait_ge(sem["mk%d" % i], 1)
            v.wait_ge(sem["md%d" % i], 1)
            v.tensor_tensor(T.tb[:, i:4 * B:4], bank(G + i), T.mk[:, _cols(i)], AluOpType.mult).then_inc(sem["tb%d" % i], 1)
    for i in range(G):
        v.wait_ge(sem["tb%d" % i], 1)
    v.quantize_mx(T.qt[:, _cols(me)], T.st[:, _cols(me)], T.tb[:, :]).then_inc(sem["q_t"], 1)
    v.wait_ge(sem["l_wv"], 32)
    v.quantize_mx(T.qwv[:, :], T.swv[:, :], T.wv[:, :]).then_inc(sem["q_wv"], 1)

    t = g.tensor
    t.wait_ge(sem["q_xe"], 1)
    for half in range(2):
        pair = (2 * half, 2 * half + 1)
        for k, s in ((0, "mu%d"), (1, "md%d")):
            for i in pair:
                if k == 0:
                    t.wait_ge(sem["q_a%d" % i], 1)
                t.matmul_mx(bank(G * k + i), T.qa[:, _cols(i)], T.sa[:, _cols(i)],
                            T.qxe[:, _cols(k)], T.sxe[:, _cols(k)], True, True).then_inc(sem[s % i], 1)
    t.wait_ge(sem["q_t"], 1)
    t.wait_ge(sem["q_wv"], 1)
    zbank = N
    lands = {r: n_near for r in peers}
    lands.update({to_relay: n_far, direct: n_far, relayed: n_all})
    for k, j in enumerate(order):
        if j != me:
            t.wait_ge(sem["arrq%d" % j], lands[j])
            t.wait_ge(sem["arrs%d" % j], lands[j])
        t.matmul_mx(bank(k), T.qwv[:, 0:B], T.swv[:, 0:B],
                    T.qt[:, _cols(j)], T.st[:, _cols(j)], True, True).then_inc(sem["ymm%d" % j], 1)
        last = k == N - 1
        m = t.matmul_mx(bank(zbank), T.qt[:, _cols(j)], T.st[:, _cols(j)],
                        T.qwv[:, B:2 * B], T.swv[:, B:2 * B], k == 0, last)
        if last:
            m.then_inc(sem["zmm"], 1)

    sent = [0]

    def send(kind, j, *parts):
        what = T.qt[:, _cols(j)].bitcast(dt.uint8) if kind == "q" else T.st[:, _cols(j)]
        g.remote_dma_fused([RemoteDMATransfer(dst_ids=[dst(r) for r in ranks], dma_engine_mask=mask,
                                              remote_sem=sem["arr%s%d" % (kind, j)],
                                              srcs=[what], dsts=[what for _ in ranks])
                            for ranks, mask in parts], local_sem=sem["sent"])
        sent[0] += sum(_popcount(mask) for _, mask in parts)
    g.wait_ge(sem["q_t"], 1)
    for kind in ("q", "s"):
        send(kind, me, ([relay], far_mask))
    for kind in ("q", "s"):
        send(kind, me, ([second], far_mask), (peers, near_mask))
    for kind in ("q", "s"):
        g.wait_ge(sem["arr%s%d" % (kind, to_relay)], n_far)
        send(kind, to_relay, ([relay_to], all_mask))

    for k, j in enumerate(order):
        v.wait_ge(sem["ymm%d" % j], 1)
        v.tensor_copy(T.ysb[:, _cols(j)], bank(k)).then_inc(sem["ycp%d" % j], 1)

    g.scalar.wait_ge(sem["ycp%d" % to_relay], 1)
    g.scalar.dma_start(T.y[:, _cols(to_relay)], T.ysb[:, _cols(to_relay)]).then_inc(sem["st_sc"], 16)
    lo, hi = here[0], here[-1] + 1
    for j in here:
        g.sync.wait_ge(sem["ycp%d" % j], 1)
    g.sync.dma_start(T.y[:, lo * B:hi * B], T.ysb[:, lo * B:hi * B]).then_inc(sem["st_sy"], 16)
    for j in (direct, relayed):
        g.sync.wait_ge(sem["ycp%d" % j], 1)
        g.sync.dma_start(T.y[:, _cols(j)], T.ysb[:, _cols(j)]).then_inc(sem["st_sy"], 16)
    g.scalar.wait_ge(sem["zmm"], 1)
    g.scalar.activation(T.zsb[:, :], bank(zbank), ActivationFunctionType.Copy).then_inc(sem["zcp"], 1)
    g.scalar.wait_ge(sem["zcp"], 1)
    g.scalar.dma_start(T.z[:, :], T.zsb[:, :]).then_inc(sem["st_sc"], 16)

    g.sync.wait_ge(sem["st_sy"], 48)
    g.scalar.wait_ge(sem["st_sc"], 32)
    g.wait_ge(sem["sent"], sent[0])
